import numpy as np
import ml_dtypes

BF16 = ml_dtypes.bfloat16


def bf(x):
    return np.asarray(x, np.float32).astype(BF16)


def f32(x):
    return np.asarray(x, np.float32)


def f64(x):
    return np.asarray(x).astype(np.float64)


def striped(idx):
    return np.tile(idx.reshape(-1, 16).T, (8, 1))


S, K, M, N, B, Q = 512, 512, 128, 128, 2, 64


def setup_inputs():
    return {"base": bf(np.random.standard_normal((B, M, S))), "x": bf(np.random.standard_normal((K, N))), "w": bf(np.random.standard_normal((K, M)) / np.sqrt(K)), "c": f32(0.2 + 0.8 * np.random.random_sample((1, S))), "offs": striped(np.random.permutation(S)[:N])}


def reference(base, x, w, c, offs):
    idx = offs[:16].T.reshape(-1)
    z = f64(base).copy()
    for i in range(B):
        z[i][:, idx[i * Q : (i + 1) * Q]] += f64(w).T @ f64(x)[:, i * Q : (i + 1) * Q]
    return z * f64(c)

@@ -1,0 +1,60 @@
+import concourse.mybir as mybir
+from concourse.masks import make_identity
+
+BF16, F32, U16 = mybir.dt.bfloat16, mybir.dt.float32, mybir.dt.uint16
+
+P = 128
+SEQS = 2
+TOKENS = 512
+K = 512
+KB = K // P
+N = 128
+PIECE = N // SEQS
+PIECE_COLS = PIECE // 16
+
+FLOPS = 2 * K * P * N
+
+
+def tile_scatter_matmul_kernel(tc, base, x, w, c, offs, out):
+    nc = tc.nc
+    with (
+        tc.tile_pool(name="held", bufs=1) as held,
+        tc.psum_pool(name="banks", bufs=1) as banks,
+    ):
+        offsets = held.tile([P, N // 16], U16, name="offsets")
+        nc.sync.dma_start(offsets[:], offs)
+
+        base_tiles = [held.tile([P, TOKENS], BF16, name="base%d" % i) for i in range(SEQS)]
+        for i in range(SEQS):
+            nc.sync.dma_start(base_tiles[i][:], base[i])
+
+        x_tile = held.tile([P, KB * N], BF16, name="x_tile")
+        w_tile = held.tile([P, KB * P], BF16, name="w_tile")
+        nc.scalar.dma_start(x_tile[:], x.rearrange("(p b) n -> p (b n)", b=KB))
+        nc.scalar.dma_start(w_tile[:], w.rearrange("(p b) m -> p (b m)", b=KB))
+
+        factors = held.tile([P, TOKENS], F32, name="factors")
+        nc.gpsimd.dma_start(factors[:], c.rearrange("o t -> (o t)").partition_broadcast(P))
+
+        identity = held.tile([P, P], BF16, name="identity")
+        make_identity(nc, identity[:])
+
+        windows = [banks.tile([P, TOKENS], F32, name="window%d" % i) for i in range(SEQS)]
+        for i in range(SEQS):
+            nc.tensor.matmul(windows[i][:], identity[:], base_tiles[i][:], start=True, stop=False)
+
+        for i in range(SEQS):
+            piece = offsets[:, i * PIECE_COLS : (i + 1) * PIECE_COLS]
+            for b in range(KB):
+                nc.tensor.matmul(
+                    windows[i][:].indirect(piece),
+                    w_tile[:, b * P : (b + 1) * P],
+                    x_tile[:, b * N + i * PIECE : b * N + (i + 1) * PIECE],
+                    start=False,
+                    stop=(b == KB - 1),
+                )
+
+        for i in range(SEQS):
+            scaled = held.tile([P, TOKENS], F32, name="scaled%d" % i)
+            nc.vector.tensor_tensor(scaled[:], windows[i][:], factors[:], mybir.AluOpType.mult)
+            nc.sync.dma_start(out[i], scaled[:])

@@ -11,6 +11,7 @@ KB = K // P
 N = 128
 PIECE = N // SEQS
 PIECE_COLS = PIECE // 16
+HALF = TOKENS // 2
 
 FLOPS = 2 * K * P * N
 
@@ -21,20 +22,20 @@ def tile_scatter_matmul_kernel(tc, base, x, w, c, offs, out):
         tc.tile_pool(name="held", bufs=1) as held,
         tc.psum_pool(name="banks", bufs=1) as banks,
     ):
+        base_tiles = [held.tile([P, TOKENS], BF16, name="base%d" % i) for i in range(SEQS)]
+        nc.sync.dma_start(base_tiles[0][:], base[0])
+        nc.scalar.dma_start(base_tiles[1][:], base[1])
+
         offsets = held.tile([P, N // 16], U16, name="offsets")
         nc.sync.dma_start(offsets[:], offs)
 
-        base_tiles = [held.tile([P, TOKENS], BF16, name="base%d" % i) for i in range(SEQS)]
-        for i in range(SEQS):
-            nc.sync.dma_start(base_tiles[i][:], base[i])
-
         x_tile = held.tile([P, KB * N], BF16, name="x_tile")
         w_tile = held.tile([P, KB * P], BF16, name="w_tile")
-        nc.scalar.dma_start(x_tile[:], x.rearrange("(p b) n -> p (b n)", b=KB))
+        nc.sync.dma_start(x_tile[:], x.rearrange("(p b) n -> p (b n)", b=KB))
         nc.scalar.dma_start(w_tile[:], w.rearrange("(p b) m -> p (b m)", b=KB))
 
         factors = held.tile([P, TOKENS], F32, name="factors")
-        nc.gpsimd.dma_start(factors[:], c.rearrange("o t -> (o t)").partition_broadcast(P))
+        nc.scalar.dma_start(factors[:], c.rearrange("o t -> (o t)").partition_broadcast(P))
 
         identity = held.tile([P, P], BF16, name="identity")
         make_identity(nc, identity[:])
@@ -55,6 +56,10 @@ def tile_scatter_matmul_kernel(tc, base, x, w, c, offs, out):
                 )
 
         for i in range(SEQS):
-            scaled = held.tile([P, TOKENS], F32, name="scaled%d" % i)
-            nc.vector.tensor_tensor(scaled[:], windows[i][:], factors[:], mybir.AluOpType.mult)
-            nc.sync.dma_start(out[i], scaled[:])
+            for h in range(2):
+                columns = slice(h * HALF, (h + 1) * HALF)
+                scaled = held.tile([P, HALF], F32, name="scaled%d_%d" % (i, h))
+                nc.vector.tensor_tensor(
+                    scaled[:], windows[i][:, columns], factors[:, columns], mybir.AluOpType.mult
+                )
+                (nc.sync, nc.scalar)[h].dma_start(out[i][:, columns], scaled[:])

@@ -11,7 +11,7 @@ KB = K // P
 N = 128
 PIECE = N // SEQS
 PIECE_COLS = PIECE // 16
-HALF = TOKENS // 2
+WARM_UPS = 2
 
 FLOPS = 2 * K * P * N
 
@@ -22,6 +22,13 @@ def tile_scatter_matmul_kernel(tc, base, x, w, c, offs, out):
         tc.tile_pool(name="held", bufs=1) as held,
         tc.psum_pool(name="banks", bufs=1) as banks,
     ):
+        c_row = held.tile([P, TOKENS], F32, name="c_row")
+        nc.gpsimd.memset(c_row[:], 0.0)
+        idle_data = held.tile([P, TOKENS], BF16, name="idle_data")
+        nc.vector.memset(idle_data[:], 0.0)
+        ones = held.tile([P, P], F32, name="ones")
+        nc.vector.memset(ones[:], 1.0)
+
         base_tiles = [held.tile([P, TOKENS], BF16, name="base%d" % i) for i in range(SEQS)]
         nc.sync.dma_start(base_tiles[0][:], base[0])
         nc.scalar.dma_start(base_tiles[1][:], base[1])
@@ -34,15 +41,23 @@ def tile_scatter_matmul_kernel(tc, base, x, w, c, offs, out):
         nc.sync.dma_start(x_tile[:], x.rearrange("(p b) n -> p (b n)", b=KB))
         nc.scalar.dma_start(w_tile[:], w.rearrange("(p b) m -> p (b m)", b=KB))
 
-        factors = held.tile([P, TOKENS], F32, name="factors")
-        nc.scalar.dma_start(factors[:], c.rearrange("o t -> (o t)").partition_broadcast(P))
+        nc.scalar.dma_start(c_row[0:1, :], c)
 
         identity = held.tile([P, P], BF16, name="identity")
         make_identity(nc, identity[:])
 
+        idle_bank = banks.tile([P, TOKENS], F32, name="idle_bank")
+        for _ in range(WARM_UPS):
+            nc.tensor.matmul(idle_bank[:], idle_data[:, 0:P], idle_data[:], start=True, stop=True)
+
         windows = [banks.tile([P, TOKENS], F32, name="window%d" % i) for i in range(SEQS)]
         for i in range(SEQS):
             nc.tensor.matmul(windows[i][:], identity[:], base_tiles[i][:], start=True, stop=False)
+
+        c_bank = banks.tile([P, TOKENS], F32, name="c_bank")
+        nc.tensor.matmul(c_bank[:], ones[:], c_row[:], start=True, stop=True)
+        factors = held.tile([P, TOKENS], F32, name="factors")
+        nc.vector.tensor_copy(factors[:], c_bank[:])
 
         for i in range(SEQS):
             piece = offsets[:, i * PIECE_COLS : (i + 1) * PIECE_COLS]
@@ -56,10 +71,6 @@ def tile_scatter_matmul_kernel(tc, base, x, w, c, offs, out):
                 )
 
         for i in range(SEQS):
-            for h in range(2):
-                columns = slice(h * HALF, (h + 1) * HALF)
-                scaled = held.tile([P, HALF], F32, name="scaled%d_%d" % (i, h))
-                nc.vector.tensor_tensor(
-                    scaled[:], windows[i][:, columns], factors[:, columns], mybir.AluOpType.mult
-                )
-                (nc.sync, nc.scalar)[h].dma_start(out[i][:, columns], scaled[:])
+            scaled = held.tile([P, TOKENS], F32, name="scaled%d" % i)
+            nc.vector.tensor_tensor(scaled[:], windows[i][:], factors[:], mybir.AluOpType.mult)
+            nc.sync.dma_start(out[i], scaled[:])

@@ -11,7 +11,7 @@ KB = K // P
 N = 128
 PIECE = N // SEQS
 PIECE_COLS = PIECE // 16
-WARM_UPS = 2
+WARM_UPS = 12
 
 FLOPS = 2 * K * P * N
 
@@ -22,12 +22,14 @@ def tile_scatter_matmul_kernel(tc, base, x, w, c, offs, out):
         tc.tile_pool(name="held", bufs=1) as held,
         tc.psum_pool(name="banks", bufs=1) as banks,
     ):
+        idle_data = held.tile([P, P], BF16, name="idle_data")
+        nc.gpsimd.memset(idle_data[:], 0.0)
         c_row = held.tile([P, TOKENS], F32, name="c_row")
         nc.gpsimd.memset(c_row[:], 0.0)
-        idle_data = held.tile([P, TOKENS], BF16, name="idle_data")
-        nc.vector.memset(idle_data[:], 0.0)
+        identity = held.tile([P, P], BF16, name="identity")
+        make_identity(nc, identity[:])
         ones = held.tile([P, P], F32, name="ones")
-        nc.vector.memset(ones[:], 1.0)
+        nc.gpsimd.memset(ones[:], 1.0)
 
         base_tiles = [held.tile([P, TOKENS], BF16, name="base%d" % i) for i in range(SEQS)]
         nc.sync.dma_start(base_tiles[0][:], base[0])
@@ -43,12 +45,9 @@ def tile_scatter_matmul_kernel(tc, base, x, w, c, offs, out):
 
         nc.scalar.dma_start(c_row[0:1, :], c)
 
-        identity = held.tile([P, P], BF16, name="identity")
-        make_identity(nc, identity[:])
-
-        idle_bank = banks.tile([P, TOKENS], F32, name="idle_bank")
-        for _ in range(WARM_UPS):
-            nc.tensor.matmul(idle_bank[:], idle_data[:, 0:P], idle_data[:], start=True, stop=True)
+        idle_bank = banks.tile([P, P], F32, name="idle_bank")
+        for warm_up in range(WARM_UPS):
+            nc.tensor.matmul(idle_bank[:], idle_data[:], idle_data[:], start=True, stop=True)
 
         windows = [banks.tile([P, TOKENS], F32, name="window%d" % i) for i in range(SEQS)]
         for i in range(SEQS):

@@ -11,7 +11,7 @@ KB = K // P
 N = 128
 PIECE = N // SEQS
 PIECE_COLS = PIECE // 16
-WARM_UPS = 12
+WARM_UPS = 24
 
 FLOPS = 2 * K * P * N
 

@@ -11,7 +11,8 @@ KB = K // P
 N = 128
 PIECE = N // SEQS
 PIECE_COLS = PIECE // 16
-WARM_UPS = 24
+C_COLS = TOKENS // P
+WARM_UPS = 20
 
 FLOPS = 2 * K * P * N
 
@@ -24,12 +25,13 @@ def tile_scatter_matmul_kernel(tc, base, x, w, c, offs, out):
     ):
         idle_data = held.tile([P, P], BF16, name="idle_data")
         nc.gpsimd.memset(idle_data[:], 0.0)
-        c_row = held.tile([P, TOKENS], F32, name="c_row")
-        nc.gpsimd.memset(c_row[:], 0.0)
+        identity_f32 = held.tile([P, P], F32, name="identity_f32")
+        make_identity(nc, identity_f32[:])
         identity = held.tile([P, P], BF16, name="identity")
         make_identity(nc, identity[:])
-        ones = held.tile([P, P], F32, name="ones")
-        nc.gpsimd.memset(ones[:], 1.0)
+
+        c_cols = held.tile([P, C_COLS], F32, name="c_cols")
+        nc.scalar.dma_start(c_cols[:], c.rearrange("o (n a) -> n (o a)", a=C_COLS))
 
         base_tiles = [held.tile([P, TOKENS], BF16, name="base%d" % i) for i in range(SEQS)]
         nc.sync.dma_start(base_tiles[0][:], base[0])
@@ -43,20 +45,26 @@ def tile_scatter_matmul_kernel(tc, base, x, w, c, offs, out):
         nc.sync.dma_start(x_tile[:], x.rearrange("(p b) n -> p (b n)", b=KB))
         nc.scalar.dma_start(w_tile[:], w.rearrange("(p b) m -> p (b m)", b=KB))
 
-        nc.scalar.dma_start(c_row[0:1, :], c)
-
         idle_bank = banks.tile([P, P], F32, name="idle_bank")
         for warm_up in range(WARM_UPS):
             nc.tensor.matmul(idle_bank[:], idle_data[:], idle_data[:], start=True, stop=True)
 
+        c_bank = banks.tile([P, TOKENS], F32, name="c_bank")
+        for a in range(C_COLS):
+            nc.tensor.transpose(
+                c_bank[:, a * P : (a + 1) * P],
+                c_cols[:, a : a + 1].to_broadcast([P, P]),
+                identity_f32[:],
+            )
+        factors = held.tile([P, TOKENS], F32, name="factors")
+        nc.vector.tensor_copy(
+            factors[:].rearrange("m (n a) -> m n a", a=C_COLS),
+            c_bank[:].rearrange("m (a n) -> m n a", a=C_COLS),
+        )
+
         windows = [banks.tile([P, TOKENS], F32, name="window%d" % i) for i in range(SEQS)]
         for i in range(SEQS):
             nc.tensor.matmul(windows[i][:], identity[:], base_tiles[i][:], start=True, stop=False)
-
-        c_bank = banks.tile([P, TOKENS], F32, name="c_bank")
-        nc.tensor.matmul(c_bank[:], ones[:], c_row[:], start=True, stop=True)
-        factors = held.tile([P, TOKENS], F32, name="factors")
-        nc.vector.tensor_copy(factors[:], c_bank[:])
 
         for i in range(SEQS):
             piece = offsets[:, i * PIECE_COLS : (i + 1) * PIECE_COLS]

@@ -12,7 +12,7 @@ N = 128
 PIECE = N // SEQS
 PIECE_COLS = PIECE // 16
 C_COLS = TOKENS // P
-WARM_UPS = 20
+WARM_UPS = 16
 
 FLOPS = 2 * K * P * N
 

@@ -31,19 +31,19 @@ def tile_scatter_matmul_kernel(tc, base, x, w, c, offs, out):
         make_identity(nc, identity[:])
 
         c_cols = held.tile([P, C_COLS], F32, name="c_cols")
-        nc.scalar.dma_start(c_cols[:], c.rearrange("o (n a) -> n (o a)", a=C_COLS))
+        nc.sync.dma_start(c_cols[:], c.rearrange("o (n a) -> n (o a)", a=C_COLS))
 
         base_tiles = [held.tile([P, TOKENS], BF16, name="base%d" % i) for i in range(SEQS)]
         nc.sync.dma_start(base_tiles[0][:], base[0])
-        nc.scalar.dma_start(base_tiles[1][:], base[1])
+        nc.sync.dma_start(base_tiles[1][:], base[1])
 
         offsets = held.tile([P, N // 16], U16, name="offsets")
         nc.sync.dma_start(offsets[:], offs)
 
         x_tile = held.tile([P, KB * N], BF16, name="x_tile")
         w_tile = held.tile([P, KB * P], BF16, name="w_tile")
+        nc.sync.dma_start(w_tile[:], w.rearrange("(p b) m -> p (b m)", b=KB))
         nc.sync.dma_start(x_tile[:], x.rearrange("(p b) n -> p (b n)", b=KB))
-        nc.scalar.dma_start(w_tile[:], w.rearrange("(p b) m -> p (b m)", b=KB))
 
         idle_bank = banks.tile([P, P], F32, name="idle_bank")
         for warm_up in range(WARM_UPS):

@@ -12,7 +12,7 @@ N = 128
 PIECE = N // SEQS
 PIECE_COLS = PIECE // 16
 C_COLS = TOKENS // P
-WARM_UPS = 16
+WARM_UPS = 12
 
 FLOPS = 2 * K * P * N
 

@@ -23,12 +23,13 @@ def tile_scatter_matmul_kernel(tc, base, x, w, c, offs, out):
         tc.tile_pool(name="held", bufs=1) as held,
         tc.psum_pool(name="banks", bufs=1) as banks,
     ):
-        idle_data = held.tile([P, P], BF16, name="idle_data")
+        idle_data = held.tile([P, 16], BF16, name="idle_data")
         nc.gpsimd.memset(idle_data[:], 0.0)
+        idle_operand = idle_data[:, 0:1].to_broadcast([P, P])
         identity_f32 = held.tile([P, P], F32, name="identity_f32")
         make_identity(nc, identity_f32[:])
         identity = held.tile([P, P], BF16, name="identity")
-        make_identity(nc, identity[:])
+        nc.vector.tensor_copy(identity[:], identity_f32[:])
 
         c_cols = held.tile([P, C_COLS], F32, name="c_cols")
         nc.sync.dma_start(c_cols[:], c.rearrange("o (n a) -> n (o a)", a=C_COLS))
@@ -47,7 +48,7 @@ def tile_scatter_matmul_kernel(tc, base, x, w, c, offs, out):
 
         idle_bank = banks.tile([P, P], F32, name="idle_bank")
         for warm_up in range(WARM_UPS):
-            nc.tensor.matmul(idle_bank[:], idle_data[:], idle_data[:], start=True, stop=True)
+            nc.tensor.matmul(idle_bank[:], idle_operand, idle_operand, start=True, stop=True)
 
         c_bank = banks.tile([P, TOKENS], F32, name="c_bank")
         for a in range(C_COLS):

@@ -8,6 +8,7 @@ SEQS = 2
 TOKENS = 512
 K = 512
 KB = K // P
+HALF_KB = KB // 2
 N = 128
 PIECE = N // SEQS
 PIECE_COLS = PIECE // 16
@@ -34,17 +35,18 @@ def tile_scatter_matmul_kernel(tc, base, x, w, c, offs, out):
         c_cols = held.tile([P, C_COLS], F32, name="c_cols")
         nc.sync.dma_start(c_cols[:], c.rearrange("o (n a) -> n (o a)", a=C_COLS))
 
-        base_tiles = [held.tile([P, TOKENS], BF16, name="base%d" % i) for i in range(SEQS)]
-        nc.sync.dma_start(base_tiles[0][:], base[0])
-        nc.sync.dma_start(base_tiles[1][:], base[1])
+        base_tile = held.tile([P, SEQS, TOKENS], BF16, name="base_tile")
+        nc.sync.dma_start(base_tile[:], base.rearrange("i m t -> m i t"))
 
         offsets = held.tile([P, N // 16], U16, name="offsets")
         nc.sync.dma_start(offsets[:], offs)
 
-        x_tile = held.tile([P, KB * N], BF16, name="x_tile")
         w_tile = held.tile([P, KB * P], BF16, name="w_tile")
         nc.sync.dma_start(w_tile[:], w.rearrange("(p b) m -> p (b m)", b=KB))
-        nc.sync.dma_start(x_tile[:], x.rearrange("(p b) n -> p (b n)", b=KB))
+        x_rows = x.rearrange("(p b) n -> p (b n)", b=KB)
+        x_halves = [held.tile([P, HALF_KB * N], BF16, name="x_half%d" % h) for h in range(2)]
+        for h in range(2):
+            nc.sync.dma_start(x_halves[h][:], x_rows[:, h * HALF_KB * N : (h + 1) * HALF_KB * N])
 
         idle_bank = banks.tile([P, P], F32, name="idle_bank")
         for warm_up in range(WARM_UPS):
@@ -65,7 +67,7 @@ def tile_scatter_matmul_kernel(tc, base, x, w, c, offs, out):
 
         windows = [banks.tile([P, TOKENS], F32, name="window%d" % i) for i in range(SEQS)]
         for i in range(SEQS):
-            nc.tensor.matmul(windows[i][:], identity[:], base_tiles[i][:], start=True, stop=False)
+            nc.tensor.matmul(windows[i][:], identity[:], base_tile[:, i, :], start=True, stop=False)
 
         for i in range(SEQS):
             piece = offsets[:, i * PIECE_COLS : (i + 1) * PIECE_COLS]
@@ -73,7 +75,7 @@ def tile_scatter_matmul_kernel(tc, base, x, w, c, offs, out):
                 nc.tensor.matmul(
                     windows[i][:].indirect(piece),
                     w_tile[:, b * P : (b + 1) * P],
-                    x_tile[:, b * N + i * PIECE : b * N + (i + 1) * PIECE],
+                    x_halves[b // HALF_KB][:, (b % HALF_KB) * N + i * PIECE : (b % HALF_KB) * N + (i + 1) * PIECE],
                     start=False,
                     stop=(b == KB - 1),
                 )

import concourse.mybir as mybir
from concourse.masks import make_identity

BF16, F32, U16 = mybir.dt.bfloat16, mybir.dt.float32, mybir.dt.uint16

P = 128
SEQS = 2
TOKENS = 512
K = 512
KB = K // P
HALF_KB = KB // 2
N = 128
PIECE = N // SEQS
PIECE_COLS = PIECE // 16
C_COLS = TOKENS // P
WARM_UPS = 12

FLOPS = 2 * K * P * N


def tile_scatter_matmul_kernel(tc, base, x, w, c, offs, out):
    nc = tc.nc
    with (
        tc.tile_pool(name="held", bufs=1) as held,
        tc.psum_pool(name="banks", bufs=1) as banks,
    ):
        idle_data = held.tile([P, 16], BF16, name="idle_data")
        nc.gpsimd.memset(idle_data[:], 0.0)
        idle_operand = idle_data[:, 0:1].to_broadcast([P, P])
        identity_f32 = held.tile([P, P], F32, name="identity_f32")
        make_identity(nc, identity_f32[:])
        identity = held.tile([P, P], BF16, name="identity")
        nc.vector.tensor_copy(identity[:], identity_f32[:])

        c_cols = held.tile([P, C_COLS], F32, name="c_cols")
        nc.sync.dma_start(c_cols[:], c.rearrange("o (n a) -> n (o a)", a=C_COLS))

        base_tile = held.tile([P, SEQS, TOKENS], BF16, name="base_tile")
        nc.sync.dma_start(base_tile[:], base.rearrange("i m t -> m i t"))

        offsets = held.tile([P, N // 16], U16, name="offsets")
        nc.sync.dma_start(offsets[:], offs)

        w_tile = held.tile([P, KB * P], BF16, name="w_tile")
        nc.sync.dma_start(w_tile[:], w.rearrange("(p b) m -> p (b m)", b=KB))
        x_rows = x.rearrange("(p b) n -> p (b n)", b=KB)
        x_halves = [held.tile([P, HALF_KB * N], BF16, name="x_half%d" % h) for h in range(2)]
        for h in range(2):
            nc.sync.dma_start(x_halves[h][:], x_rows[:, h * HALF_KB * N : (h + 1) * HALF_KB * N])

        idle_bank = banks.tile([P, P], F32, name="idle_bank")
        for warm_up in range(WARM_UPS):
            nc.tensor.matmul(idle_bank[:], idle_operand, idle_operand, start=True, stop=True)

        c_bank = banks.tile([P, TOKENS], F32, name="c_bank")
        for a in range(C_COLS):
            nc.tensor.transpose(
                c_bank[:, a * P : (a + 1) * P],
                c_cols[:, a : a + 1].to_broadcast([P, P]),
                identity_f32[:],
            )
        factors = held.tile([P, TOKENS], F32, name="factors")
        nc.vector.tensor_copy(
            factors[:].rearrange("m (n a) -> m n a", a=C_COLS),
            c_bank[:].rearrange("m (a n) -> m n a", a=C_COLS),
        )

        windows = [banks.tile([P, TOKENS], F32, name="window%d" % i) for i in range(SEQS)]
        for i in range(SEQS):
            nc.tensor.matmul(windows[i][:], identity[:], base_tile[:, i, :], start=True, stop=False)

        for i in range(SEQS):
            piece = offsets[:, i * PIECE_COLS : (i + 1) * PIECE_COLS]
            for b in range(KB):
                nc.tensor.matmul(
                    windows[i][:].indirect(piece),
                    w_tile[:, b * P : (b + 1) * P],
                    x_halves[b // HALF_KB][:, (b % HALF_KB) * N + i * PIECE : (b % HALF_KB) * N + (i + 1) * PIECE],
                    start=False,
                    stop=(b == KB - 1),
                )

        for i in range(SEQS):
            scaled = held.tile([P, TOKENS], F32, name="scaled%d" % i)
            nc.vector.tensor_tensor(scaled[:], windows[i][:], factors[:], mybir.AluOpType.mult)
            nc.sync.dma_start(out[i], scaled[:])
